import numpy as np
import ml_dtypes


def mxq(x, axis, fmt="e4m3"):
    dtype, down = {"e4m3": (ml_dtypes.float8_e4m3fn, 7), "e5m2": (ml_dtypes.float8_e5m2, 14)}[fmt]
    v = np.moveaxis(np.asarray(x, np.float32).astype(ml_dtypes.bfloat16).astype(np.float64), axis, -1)
    blocks = v.reshape(v.shape[:-1] + (-1, 32))
    amax = np.abs(blocks).max(-1, keepdims=True)
    byte = np.maximum(np.where(amax > 0, np.frexp(amax)[1] - 1 + 127, 0) - down, 1)
    scale = np.exp2(byte - 127.0)
    codes = (blocks / scale).astype(np.float32).astype(dtype).astype(np.float64)
    return np.moveaxis((codes * scale).reshape(v.shape), -1, axis)


WIDE = False


def mx_kscale(k):
    if not WIDE:
        return np.ones(k)
    levels = np.array([10, -10, 5, -5, 0])
    if k % 512:
        return np.exp2(np.random.permutation(np.resize(levels, k // 32))).repeat(32)
    a = np.empty((k // 512, 16))
    for p in range(k // 512):
        a[p, :8] = np.random.permutation(np.resize(levels, 8))
        for g in range(8):
            far = levels[np.abs(levels - a[p, g]) >= 10]
            a[p, g + 8] = far[np.random.randint(len(far))]
    return np.exp2(a.ravel()).repeat(32)


def f64(x):
    return np.asarray(x).astype(np.float64)


def striped(idx):
    return np.tile(idx.reshape(-1, 16).T, (8, 1)).astype(np.uint16)


def unstriped(offs):
    return offs[:16].T.reshape(-1).astype(np.int64)


E2M1 = np.array([0.0, 0.5, 1.0, 1.5, 2.0, 3.0, 4.0, 6.0, -0.0, -0.5, -1.0, -1.5, -2.0, -3.0, -4.0, -6.0])


def pack_weight(w, fmt):
    k, n = w.shape
    w = f64(np.asarray(w, np.float32).astype(ml_dtypes.bfloat16)).reshape(k // 32, 32, n)
    amax = np.abs(w).max(1)
    if fmt == "e4m3":
        byte = np.frexp(amax)[1] - 1 + 127 - 7
    else:
        mant, ex = np.frexp(amax / 6.0)
        byte = np.where(mant > 0.5, ex, ex - 1) + 127
    byte = np.clip(np.where(amax > 0, byte, 1), 1, 254)
    scaled = (w * np.exp2(127.0 - byte)[:, None, :]).reshape(k, n).astype(np.float32)
    by_word = np.ascontiguousarray(scaled.reshape(k // 512, 128, 4, n).transpose(0, 1, 3, 2))
    if fmt == "e4m3":
        words = by_word.astype(ml_dtypes.float8_e4m3fn).view(np.uint8)
    else:
        c = by_word.astype(ml_dtypes.float4_e2m1fn).view(np.uint8) & 0xF
        words = (c[..., 0::2] | (c[..., 1::2] << 4)).reshape(k // 512, 128, 2 * n)
    return np.ascontiguousarray(words), np.ascontiguousarray(byte.astype(np.uint8).reshape(k // 512, 16, n))


def unpack_weight(words, scales, fmt):
    g, _, n = scales.shape
    words = np.ascontiguousarray(words).reshape(g, 128, n, -1)
    if fmt == "e4m3":
        vals = words.view(ml_dtypes.float8_e4m3fn).astype(np.float64)
    else:
        nib = np.empty((g, 128, n, 4), np.uint8)
        nib[..., 0::2] = words & 0xF
        nib[..., 1::2] = words >> 4
        vals = E2M1[nib]
    vals = vals * np.repeat(np.exp2(scales.astype(np.float64) - 127.0), 8, axis=1)[..., None]
    return vals.transpose(0, 1, 3, 2).reshape(g * 512, n)


def d_relu2(v):
    return 2.0 * np.maximum(v, 0.0)


K, T, E, C, H, N = 512, 512, 4, 128, 512, 1024


def by_expert(wq, xq):
    return np.concatenate([wq[e].T @ xq[:, e * C:(e + 1) * C] for e in range(E)], axis=1)


def setup_inputs():
    n = np.random.standard_normal
    s = mx_kscale(K)
    v = mx_kscale(N)
    u = mx_kscale(H)
    slot_token = np.random.permutation(T)[:E * C]
    w_slot = np.random.uniform(0.2, 1.0, E * C)
    x = pack_weight(n((K, T)) * s[:, None], "e4m3")
    dy = pack_weight(n((N, T)) * v[:, None], "e4m3")
    m1 = n((E, K, H))
    w1 = [pack_weight(m, "e4m3") for m in m1 / np.sqrt(K) / s[None, :, None]]
    w2t = [pack_weight(m, "e4m3") for m in n((E, N, H)) / np.sqrt(N) / v[None, :, None] * u]
    w1t = [pack_weight(m, "e4m3") for m in m1.transpose(0, 2, 1) / np.sqrt(H) / u[None, :, None]]
    return {
        "x_words": x[0],
        "x_scales": x[1],
        "dy_words": dy[0],
        "dy_scales": dy[1],
        "w1_words": np.stack([m[0] for m in w1]),
        "w1_scales": np.stack([m[1] for m in w1]),
        "w2t_words": np.stack([m[0] for m in w2t]),
        "w2t_scales": np.stack([m[1] for m in w2t]),
        "w1t_words": np.stack([m[0] for m in w1t]),
        "w1t_scales": np.stack([m[1] for m in w1t]),
        "gate": (np.tile(w_slot, (128, 1))).astype(np.float32),
        "offs": striped(slot_token),
    }


def reference(x_words, x_scales, dy_words, dy_scales, w1_words, w1_scales, w2t_words, w2t_scales, w1t_words, w1t_scales, gate, offs):
    w1 = np.stack([unpack_weight(w1_words[e], w1_scales[e], "e4m3") for e in range(E)])
    w2t = np.stack([unpack_weight(w2t_words[e], w2t_scales[e], "e4m3") for e in range(E)])
    w1t = np.stack([unpack_weight(w1t_words[e], w1t_scales[e], "e4m3") for e in range(E)])
    idx = unstriped(offs)
    xq = unpack_weight(x_words, x_scales, "e4m3")[:, idx]
    gq = unpack_weight(dy_words, dy_scales, "e4m3")[:, idx]
    dh = f64(gate[:1]) * by_expert(w2t, gq)
    a = by_expert(w1, xq)
    dx = by_expert(w1t, mxq(dh * d_relu2(a), 0, "e4m3"))
    out = np.zeros((K, T))
    out[:, idx] = dx
    return out

@@ -1,0 +1,197 @@
+from contextlib import ExitStack
+
+import concourse.mybir as mybir
+from concourse.masks import make_identity
+
+K, T, E, C, H, N = 512, 512, 4, 128, 512, 1024
+FLOPS = 2 * E * C * (K * H + N * H + H * K)
+
+F32 = mybir.dt.float32
+BF16 = mybir.dt.bfloat16
+I32 = mybir.dt.int32
+U32 = mybir.dt.uint32
+U16 = mybir.dt.uint16
+U8 = mybir.dt.uint8
+FP8X4 = mybir.dt.float8_e4m3fn_x4
+MULT = mybir.AluOpType.mult
+RELU = mybir.ActivationFunctionType.Relu
+COPY = mybir.ActivationFunctionType.Copy
+
+P = 128
+S = E * C
+N_PASSES = N // 512
+K_BLOCKS = K // P
+
+
+def tile_moe_rec_mlp_relu2_kernel(
+    tc, x_words, x_scales, dy_words, dy_scales, w1_words, w1_scales,
+    w2t_words, w2t_scales, w1t_words, w1t_scales, gate, offs, out,
+):
+    nc = tc.nc
+
+    with ExitStack() as ctx:
+        keep = ctx.enter_context(tc.tile_pool(name="keep", bufs=1))
+        ring = ctx.enter_context(tc.tile_pool(name="ring", bufs=2))
+        psum = ctx.enter_context(tc.psum_pool(name="psum", bufs=1))
+
+        offsets = keep.tile([P, S // 16], U16, name="offsets")
+
+        def plane(name, engine):
+            t = keep.tile([P, 512], U8, name=name, align_bytes=64)
+            engine.memset(t[:].bitcast(I32), 0)
+            return t
+
+        def load_plane(t, rows, quadrants):
+            n = rows.shape[0]
+            for q in quadrants:
+                nc.sync.dma_start(
+                    out=t[32 * q : 32 * q + 4 * n, :].bitcast(I32),
+                    in_=rows[:, 4 * q : 4 * q + 4, :].bitcast(I32),
+                )
+
+        def load_words(name, words, dtype):
+            n = words.shape[0]
+            t = keep.tile([P, n * 512], dtype, name=name, align_bytes=64)
+            nc.sync.dma_start(
+                out=t[:].bitcast(I32).rearrange("p (s c) -> p s c", s=n),
+                in_=words.rearrange("s p c d -> p s (c d)").bitcast(I32),
+            )
+            return t
+
+        x_plane = keep.tile([P, 512], U8, name="x_plane", align_bytes=64)
+        dy_plane = plane("dy_plane", nc.gpsimd)
+        w1_plane = plane("w1_plane", nc.gpsimd)
+        w2_planes = [plane(f"w2_plane{h}", nc.gpsimd) for h in range(2)]
+        w1t_plane = plane("w1t_plane", nc.gpsimd)
+        identity = keep.tile([P, P], F32, name="identity")
+        make_identity(nc, identity[:])
+
+        nc.sync.dma_start(offsets[:], offs)
+        x_all = load_words("x_all", x_words, I32)
+        for q in range(4):
+            nc.sync.dma_start(
+                out=x_plane[32 * q : 32 * q + 32, :].bitcast(I32),
+                in_=x_scales[0, 4 * q : 4 * q + 4, :].bitcast(I32).partition_broadcast(8),
+            )
+        dy_all = load_words("dy_all", dy_words, I32)
+        w1, w2, w1t = [], [], []
+        w1.append(load_words("w1_0", w1_words[0], U32))
+        load_plane(dy_plane, dy_scales, range(4))
+        w1_rows = w1_scales.rearrange("e s b c -> (e s) b c")
+        w2_rows = w2t_scales.rearrange("e s b c -> (e s) b c")
+        load_plane(w1_plane, w1_rows, range(2))
+        w2.append(load_words("w2_0", w2t_words[0], U32))
+        load_plane(w1_plane, w1_rows, range(2, 4))
+        load_plane(w2_planes[0], w2_rows[0:4], range(4))
+        gate_rows = keep.tile([P, C], F32, name="gate_rows")
+        nc.sync.dma_start(out=gate_rows[:], in_=gate[: P // E, :].rearrange("r (e c) -> (r e) c", e=E))
+        w1t.append(load_words("w1t_0", w1t_words[0], U32))
+        load_plane(w1t_plane, w1t_scales.rearrange("e s b c -> (e s) b c"), range(4))
+        for e in range(1, E):
+            w2.append(load_words(f"w2_{e}", w2t_words[e], U32))
+            if e == 2:
+                load_plane(w2_planes[1], w2_rows[4:8], range(4))
+            w1.append(load_words(f"w1_{e}", w1_words[e], U32))
+            w1t.append(load_words(f"w1t_{e}", w1t_words[e], U32))
+
+        gate_ps = psum.tile([P, 2, P], F32, name="gate_ps", tag="bank_t3")
+        nc.tensor.transpose(gate_ps[:, 0, :], gate_rows[:], identity[:])
+        gate_col = keep.tile([P, E], F32, name="gate_col")
+        nc.scalar.activation(gate_col[:], gate_ps[:, 0, 0:E], COPY)
+
+        def gather(part, lo, hi):
+            lst = offsets[:, lo // 16 : hi // 16]
+            n = hi - lo
+            held = part == "rest"
+            x_g = keep.tile([P, n], U32, name=f"x_{part}", tag=f"x_{part}", align_bytes=64)
+            xs_g = keep.tile([P, n], U8, name=f"xs_{part}", align_bytes=64)
+            dys_g = keep.tile([P, n], U8, name=f"dys_{part}", align_bytes=64)
+            nc.vector.tensor_copy(x_g[:], x_all[:].bitcast(U32).indirect(lst))
+            nc.vector.tensor_copy(xs_g[:], x_plane[:].indirect(lst))
+            nc.vector.tensor_copy(dys_g[:], dy_plane[:].indirect(lst))
+            dy_g = {}
+            for s in range(1 if held else N_PASSES):
+                dy_g[s] = gather_dy(s, f"dy{s}_{part}", lo, hi)
+            return x_g, xs_g, dy_g, dys_g
+
+        def gather_dy(s, tag, lo, hi):
+            t = keep.tile([P, hi - lo], U32, name=f"dy{s}_{lo}", tag=tag, align_bytes=64)
+            nc.vector.tensor_copy(
+                t[:], dy_all[:, s * T : (s + 1) * T].bitcast(U32).indirect(offsets[:, lo // 16 : hi // 16])
+            )
+            return t
+
+        first = gather("first", 0, C)
+        rest = gather("rest", C, S)
+
+        dx_tokens = [keep.tile([P, T], F32, name=f"dx_tokens{b}") for b in range(K_BLOCKS)]
+        da_t, dx_ps = {}, {}
+
+        def front(e):
+            x_g, xs_g, dy_g, dys_g = first if e == 0 else rest
+            slots = slice(0, C) if e == 0 else slice((e - 1) * C, e * C)
+            a_ps = psum.tile([P, H], F32, name="a_ps", tag=f"bank_a{e % 2}")
+            nc.tensor.matmul_mx(
+                out=a_ps[:], lhsT=x_g[:, slots].bitcast(FP8X4), lhsT_scale=xs_g[:, slots],
+                rhs=w1[e][:].bitcast(FP8X4), rhs_scale=w1_plane[4 * e :, :], start=True, stop=True,
+            )
+            dh_ps = psum.tile([P, H], F32, name="dh_ps", tag=f"bank_dh{e % 2}")
+            for s in range(N_PASSES):
+                nc.tensor.matmul_mx(
+                    out=dh_ps[:], lhsT=dy_g[s][:, slots].bitcast(FP8X4), lhsT_scale=dys_g[4 * s :, slots],
+                    rhs=w2[e][:, s * H : (s + 1) * H].bitcast(FP8X4),
+                    rhs_scale=w2_planes[e // 2][4 * (2 * (e % 2) + s) :, :],
+                    start=(s == 0), stop=(s == N_PASSES - 1),
+                )
+            slope = ring.tile([P, H], F32, name="slope")
+            nc.scalar.activation(slope[:], a_ps[:], RELU, scale=2.0)
+            da_t[e] = keep.tile([P, H], BF16, name=f"da_t{e}", tag=f"da_t{e}")
+            nc.vector.scalar_tensor_tensor(da_t[e][:], dh_ps[:], gate_col[:, e : e + 1], slope[:], MULT, MULT)
+
+        def hand_out(e, half):
+            tag = f"da_t{e + 1}" if half == 1 and e + 1 < E else f"dx_{e}_{half}"
+            staged = keep.tile([P, 2, C], F32, name=f"dx_{e}_{half}", tag=tag)
+            nc.scalar.copy(staged[:], dx_ps[e][:, 2 * half : 2 * half + 2, :])
+            for i in range(2):
+                b = 2 * half + i
+                nc.vector.tensor_copy(
+                    dx_tokens[b][:].indirect(offsets[:, e * C // 16 : (e + 1) * C // 16]), staged[:, i, :]
+                )
+                if e == E - 1:
+                    nc.sync.dma_start(out=out[b * P : (b + 1) * P, :], in_=dx_tokens[b][:])
+
+        def back(e):
+            pairs = da_t[e][:].bitcast(F32)
+            tag = f"bank_a{(e + 1) % 2}" if 0 < e < E - 1 else f"bank_t{e}"
+            turned = psum.tile([P, 2, P], F32, name="turned", tag=tag)
+            for u in range(2):
+                nc.tensor.transpose(turned[:, u, :], pairs[:, u : H // 2 : 2], identity[:])
+            da = ring.tile([P, 4 * C], BF16, name="da", align_bytes=64)
+            nc.scalar.copy(
+                da[:].bitcast(F32).rearrange("p (j u) -> p j u", u=2), turned[:].rearrange("p u j -> p j u")
+            )
+            da_q = ring.tile([P, C], U32, name="da_q", align_bytes=64)
+            da_s = ring.tile([P, C], U8, name="da_s", align_bytes=64)
+            nc.vector.quantize_mx(out=da_q[:].bitcast(FP8X4), scales=da_s[:], in_=da[:])
+            dx_ps[e] = psum.tile([P, K_BLOCKS, C], F32, name="dx_ps", tag=f"bank_dx{e % 2}")
+            for b in range(K_BLOCKS):
+                cols = slice(b * P, (b + 1) * P)
+                nc.tensor.matmul_mx(
+                    out=dx_ps[e][:, b, :], lhsT=w1t[e][:, cols].bitcast(FP8X4),
+                    lhsT_scale=w1t_plane[4 * e :, cols],
+                    rhs=da_q[:].bitcast(FP8X4), rhs_scale=da_s[:], start=True, stop=True,
+                )
+            if e > 0:
+                hand_out(e - 1, 1)
+            hand_out(e, 0)
+
+        front(0)
+        rest[2][1] = gather_dy(1, "x_first", C, S)
+        back(0)
+        front(1)
+        front(2)
+        back(1)
+        front(3)
+        back(2)
+        back(3)
+        hand_out(E - 1, 1)

@@ -41,7 +41,7 @@ def tile_moe_rec_mlp_relu2_kernel(
             engine.memset(t[:].bitcast(I32), 0)
             return t
 
-        def load_plane(t, rows, quadrants):
+        def load_plane(t, rows, quadrants=range(4)):
             n = rows.shape[0]
             for q in quadrants:
                 nc.sync.dma_start(
@@ -65,6 +65,8 @@ def tile_moe_rec_mlp_relu2_kernel(
         w1t_plane = plane("w1t_plane", nc.gpsimd)
         identity = keep.tile([P, P], F32, name="identity")
         make_identity(nc, identity[:])
+        w1_rows = w1_scales.rearrange("e s b c -> (e s) b c")
+        w2_rows = w2t_scales.rearrange("e s b c -> (e s) b c")
 
         nc.sync.dma_start(offsets[:], offs)
         x_all = load_words("x_all", x_words, I32)
@@ -76,22 +78,21 @@ def tile_moe_rec_mlp_relu2_kernel(
         dy_all = load_words("dy_all", dy_words, I32)
         w1, w2, w1t = [], [], []
         w1.append(load_words("w1_0", w1_words[0], U32))
-        load_plane(dy_plane, dy_scales, range(4))
-        w1_rows = w1_scales.rearrange("e s b c -> (e s) b c")
-        w2_rows = w2t_scales.rearrange("e s b c -> (e s) b c")
-        load_plane(w1_plane, w1_rows, range(2))
-        w2.append(load_words("w2_0", w2t_words[0], U32))
-        load_plane(w1_plane, w1_rows, range(2, 4))
-        load_plane(w2_planes[0], w2_rows[0:4], range(4))
         gate_rows = keep.tile([P, C], F32, name="gate_rows")
         nc.sync.dma_start(out=gate_rows[:], in_=gate[: P // E, :].rearrange("r (e c) -> (r e) c", e=E))
-        w1t.append(load_words("w1t_0", w1t_words[0], U32))
-        load_plane(w1t_plane, w1t_scales.rearrange("e s b c -> (e s) b c"), range(4))
+        load_plane(dy_plane, dy_scales)
+        load_plane(w1_plane, w1_rows, range(1))
+        w2.append(load_words("w2_0", w2t_words[0], U32))
+        load_plane(w1_plane, w1_rows, range(1, 4))
+        load_plane(w2_planes[0], w2_rows[0:4])
         for e in range(1, E):
             w2.append(load_words(f"w2_{e}", w2t_words[e], U32))
             if e == 2:
-                load_plane(w2_planes[1], w2_rows[4:8], range(4))
+                load_plane(w2_planes[1], w2_rows[4:8])
             w1.append(load_words(f"w1_{e}", w1_words[e], U32))
+            if e == 1:
+                load_plane(w1t_plane, w1t_scales.rearrange("e s b c -> (e s) b c"))
+                w1t.append(load_words("w1t_0", w1t_words[0], U32))
             w1t.append(load_words(f"w1t_{e}", w1t_words[e], U32))
 
         gate_ps = psum.tile([P, 2, P], F32, name="gate_ps", tag="bank_t3")
@@ -99,36 +100,32 @@ def tile_moe_rec_mlp_relu2_kernel(
         gate_col = keep.tile([P, E], F32, name="gate_col")
         nc.scalar.activation(gate_col[:], gate_ps[:, 0, 0:E], COPY)
 
-        def gather(part, lo, hi):
-            lst = offsets[:, lo // 16 : hi // 16]
-            n = hi - lo
-            held = part == "rest"
-            x_g = keep.tile([P, n], U32, name=f"x_{part}", tag=f"x_{part}", align_bytes=64)
-            xs_g = keep.tile([P, n], U8, name=f"xs_{part}", align_bytes=64)
-            dys_g = keep.tile([P, n], U8, name=f"dys_{part}", align_bytes=64)
-            nc.vector.tensor_copy(x_g[:], x_all[:].bitcast(U32).indirect(lst))
-            nc.vector.tensor_copy(xs_g[:], x_plane[:].indirect(lst))
-            nc.vector.tensor_copy(dys_g[:], dy_plane[:].indirect(lst))
-            dy_g = {}
-            for s in range(1 if held else N_PASSES):
-                dy_g[s] = gather_dy(s, f"dy{s}_{part}", lo, hi)
-            return x_g, xs_g, dy_g, dys_g
+        windows = {
+            "x": (x_all[:].bitcast(U32), U32),
+            "xs": (x_plane[:], U8),
+            "dys": (dy_plane[:], U8),
+            "dy0": (dy_all[:, 0:T].bitcast(U32), U32),
+            "dy1": (dy_all[:, T : 2 * T].bitcast(U32), U32),
+        }
+        first, rest = {}, {}
 
-        def gather_dy(s, tag, lo, hi):
-            t = keep.tile([P, hi - lo], U32, name=f"dy{s}_{lo}", tag=tag, align_bytes=64)
-            nc.vector.tensor_copy(
-                t[:], dy_all[:, s * T : (s + 1) * T].bitcast(U32).indirect(offsets[:, lo // 16 : hi // 16])
-            )
-            return t
+        def gather(part, sort, tag, lo, hi):
+            window, dtype = windows[sort]
+            part[sort] = keep.tile([P, hi - lo], dtype, name=f"{sort}_{lo}", tag=tag, align_bytes=64)
+            nc.vector.tensor_copy(part[sort][:], window.indirect(offsets[:, lo // 16 : hi // 16]))
 
-        first = gather("first", 0, C)
-        rest = gather("rest", C, S)
+        for sort in windows:
+            gather(first, sort, f"{sort}_first", 0, C)
+        for sort in ("x", "dy0", "dy1", "dys"):
+            gather(rest, sort, f"{sort}_rest", C, S)
 
         dx_tokens = [keep.tile([P, T], F32, name=f"dx_tokens{b}") for b in range(K_BLOCKS)]
         da_t, dx_ps = {}, {}
 
         def front(e):
-            x_g, xs_g, dy_g, dys_g = first if e == 0 else rest
+            part = first if e == 0 else rest
+            x_g, xs_g, dys_g = part["x"], part["xs"], part["dys"]
+            dy_g = [part["dy0"], part["dy1"]]
             slots = slice(0, C) if e == 0 else slice((e - 1) * C, e * C)
             a_ps = psum.tile([P, H], F32, name="a_ps", tag=f"bank_a{e % 2}")
             nc.tensor.matmul_mx(
@@ -143,7 +140,7 @@ def tile_moe_rec_mlp_relu2_kernel(
                     rhs_scale=w2_planes[e // 2][4 * (2 * (e % 2) + s) :, :],
                     start=(s == 0), stop=(s == N_PASSES - 1),
                 )
-            slope = ring.tile([P, H], F32, name="slope")
+            slope = keep.tile([P, H], F32, name=f"slope{e}", tag=f"slope{e}", align_bytes=64)
             nc.scalar.activation(slope[:], a_ps[:], RELU, scale=2.0)
             da_t[e] = keep.tile([P, H], BF16, name=f"da_t{e}", tag=f"da_t{e}")
             nc.vector.scalar_tensor_tensor(da_t[e][:], dh_ps[:], gate_col[:, e : e + 1], slope[:], MULT, MULT)
@@ -151,7 +148,7 @@ def tile_moe_rec_mlp_relu2_kernel(
         def hand_out(e, half):
             tag = f"da_t{e + 1}" if half == 1 and e + 1 < E else f"dx_{e}_{half}"
             staged = keep.tile([P, 2, C], F32, name=f"dx_{e}_{half}", tag=tag)
-            nc.scalar.copy(staged[:], dx_ps[e][:, 2 * half : 2 * half + 2, :])
+            nc.scalar.copy(staged[:], dx_ps[e][half][:])
             for i in range(2):
                 b = 2 * half + i
                 nc.vector.tensor_copy(
@@ -173,20 +170,20 @@ def tile_moe_rec_mlp_relu2_kernel(
             da_q = ring.tile([P, C], U32, name="da_q", align_bytes=64)
             da_s = ring.tile([P, C], U8, name="da_s", align_bytes=64)
             nc.vector.quantize_mx(out=da_q[:].bitcast(FP8X4), scales=da_s[:], in_=da[:])
-            dx_ps[e] = psum.tile([P, K_BLOCKS, C], F32, name="dx_ps", tag=f"bank_dx{e % 2}")
+            if e > 0:
+                hand_out(e - 1, 1)
+            dx_ps[e] = [psum.tile([P, 2, C], F32, name=f"dx_ps{h}", tag=f"bank_dx{h}") for h in range(2)]
             for b in range(K_BLOCKS):
                 cols = slice(b * P, (b + 1) * P)
                 nc.tensor.matmul_mx(
-                    out=dx_ps[e][:, b, :], lhsT=w1t[e][:, cols].bitcast(FP8X4),
+                    out=dx_ps[e][b // 2][:, b % 2, :], lhsT=w1t[e][:, cols].bitcast(FP8X4),
                     lhsT_scale=w1t_plane[4 * e :, cols],
                     rhs=da_q[:].bitcast(FP8X4), rhs_scale=da_s[:], start=True, stop=True,
                 )
-            if e > 0:
-                hand_out(e - 1, 1)
             hand_out(e, 0)
 
         front(0)
-        rest[2][1] = gather_dy(1, "x_first", C, S)
+        gather(rest, "xs", "slope0", C, S)
         back(0)
         front(1)
         front(2)

@@ -41,10 +41,10 @@ def tile_moe_rec_mlp_relu2_kernel(
             engine.memset(t[:].bitcast(I32), 0)
             return t
 
-        def load_plane(t, rows, quadrants=range(4)):
+        def load_plane(t, rows, quadrants=range(4), engine=nc.sync):
             n = rows.shape[0]
             for q in quadrants:
-                nc.sync.dma_start(
+                engine.dma_start(
                     out=t[32 * q : 32 * q + 4 * n, :].bitcast(I32),
                     in_=rows[:, 4 * q : 4 * q + 4, :].bitcast(I32),
                 )
@@ -61,12 +61,18 @@ def tile_moe_rec_mlp_relu2_kernel(
         x_plane = keep.tile([P, 512], U8, name="x_plane", align_bytes=64)
         dy_plane = plane("dy_plane", nc.gpsimd)
         w1_plane = plane("w1_plane", nc.gpsimd)
-        w2_planes = [plane(f"w2_plane{h}", nc.gpsimd) for h in range(2)]
-        w1t_plane = plane("w1t_plane", nc.gpsimd)
-        identity = keep.tile([P, P], F32, name="identity")
-        make_identity(nc, identity[:])
+        w2_planes = [plane("w2_plane0", nc.gpsimd)]
         w1_rows = w1_scales.rearrange("e s b c -> (e s) b c")
         w2_rows = w2t_scales.rearrange("e s b c -> (e s) b c")
+        gate_rows = keep.tile([P, C], F32, name="gate_rows")
+        nc.gpsimd.dma_start(out=gate_rows[:], in_=gate[: P // E, :].rearrange("r (e c) -> (r e) c", e=E))
+        identity = keep.tile([P, P], F32, name="identity")
+        nc.vector.memset(identity[:], 0.0)
+        make_identity(nc, identity[:], nomemset=True)
+        load_plane(w2_planes[0], w2_rows[0:4], engine=nc.gpsimd)
+
+        w1t_plane = plane("w1t_plane", nc.vector)
+        w2_planes.append(plane("w2_plane1", nc.vector))
 
         nc.sync.dma_start(offsets[:], offs)
         x_all = load_words("x_all", x_words, I32)
@@ -78,24 +84,21 @@ def tile_moe_rec_mlp_relu2_kernel(
         dy_all = load_words("dy_all", dy_words, I32)
         w1, w2, w1t = [], [], []
         w1.append(load_words("w1_0", w1_words[0], U32))
-        gate_rows = keep.tile([P, C], F32, name="gate_rows")
-        nc.sync.dma_start(out=gate_rows[:], in_=gate[: P // E, :].rearrange("r (e c) -> (r e) c", e=E))
         load_plane(dy_plane, dy_scales)
         load_plane(w1_plane, w1_rows, range(1))
         w2.append(load_words("w2_0", w2t_words[0], U32))
         load_plane(w1_plane, w1_rows, range(1, 4))
-        load_plane(w2_planes[0], w2_rows[0:4])
         for e in range(1, E):
             w2.append(load_words(f"w2_{e}", w2t_words[e], U32))
+            w1.append(load_words(f"w1_{e}", w1_words[e], U32))
             if e == 2:
                 load_plane(w2_planes[1], w2_rows[4:8])
-            w1.append(load_words(f"w1_{e}", w1_words[e], U32))
+            w1t.append(load_words(f"w1t_{e - 1}", w1t_words[e - 1], U32))
             if e == 1:
                 load_plane(w1t_plane, w1t_scales.rearrange("e s b c -> (e s) b c"))
-                w1t.append(load_words("w1t_0", w1t_words[0], U32))
-            w1t.append(load_words(f"w1t_{e}", w1t_words[e], U32))
+        w1t.append(load_words(f"w1t_{E - 1}", w1t_words[E - 1], U32))
 
-        gate_ps = psum.tile([P, 2, P], F32, name="gate_ps", tag="bank_t3")
+        gate_ps = psum.tile([P, 2, P], F32, name="gate_ps", tag="bank_t1")
         nc.tensor.transpose(gate_ps[:, 0, :], gate_rows[:], identity[:])
         gate_col = keep.tile([P, E], F32, name="gate_col")
         nc.scalar.activation(gate_col[:], gate_ps[:, 0, 0:E], COPY)
@@ -127,12 +130,12 @@ def tile_moe_rec_mlp_relu2_kernel(
             x_g, xs_g, dys_g = part["x"], part["xs"], part["dys"]
             dy_g = [part["dy0"], part["dy1"]]
             slots = slice(0, C) if e == 0 else slice((e - 1) * C, e * C)
-            a_ps = psum.tile([P, H], F32, name="a_ps", tag=f"bank_a{e % 2}")
+            a_ps = psum.tile([P, H], F32, name="a_ps", tag="first_half1" if e == 0 else "second_half")
             nc.tensor.matmul_mx(
                 out=a_ps[:], lhsT=x_g[:, slots].bitcast(FP8X4), lhsT_scale=xs_g[:, slots],
                 rhs=w1[e][:].bitcast(FP8X4), rhs_scale=w1_plane[4 * e :, :], start=True, stop=True,
             )
-            dh_ps = psum.tile([P, H], F32, name="dh_ps", tag=f"bank_dh{e % 2}")
+            dh_ps = psum.tile([P, H], F32, name="dh_ps", tag=f"dh{e}" if e < 2 else f"first_half{e % 2}")
             for s in range(N_PASSES):
                 nc.tensor.matmul_mx(
                     out=dh_ps[:], lhsT=dy_g[s][:, slots].bitcast(FP8X4), lhsT_scale=dys_g[4 * s :, slots],
@@ -157,10 +160,11 @@ def tile_moe_rec_mlp_relu2_kernel(
                 if e == E - 1:
                     nc.sync.dma_start(out=out[b * P : (b + 1) * P, :], in_=dx_tokens[b][:])
 
-        def back(e):
+        da_mx = {}
+
+        def turn(e):
             pairs = da_t[e][:].bitcast(F32)
-            tag = f"bank_a{(e + 1) % 2}" if 0 < e < E - 1 else f"bank_t{e}"
-            turned = psum.tile([P, 2, P], F32, name="turned", tag=tag)
+            turned = psum.tile([P, 2, P], F32, name="turned", tag="second_half" if e == 0 else f"bank_t{e % 2}")
             for u in range(2):
                 nc.tensor.transpose(turned[:, u, :], pairs[:, u : H // 2 : 2], identity[:])
             da = ring.tile([P, 4 * C], BF16, name="da", align_bytes=64)
@@ -170,25 +174,30 @@ def tile_moe_rec_mlp_relu2_kernel(
             da_q = ring.tile([P, C], U32, name="da_q", align_bytes=64)
             da_s = ring.tile([P, C], U8, name="da_s", align_bytes=64)
             nc.vector.quantize_mx(out=da_q[:].bitcast(FP8X4), scales=da_s[:], in_=da[:])
-            if e > 0:
-                hand_out(e - 1, 1)
-            dx_ps[e] = [psum.tile([P, 2, C], F32, name=f"dx_ps{h}", tag=f"bank_dx{h}") for h in range(2)]
-            for b in range(K_BLOCKS):
-                cols = slice(b * P, (b + 1) * P)
+            da_mx[e] = (da_q, da_s)
+            dx_ps[e] = {}
+
+        def back(e, half):
+            da_q, da_s = da_mx[e]
+            tag = "second_half" if half == 1 else f"first_half{e % 2}"
+            dx_ps[e][half] = psum.tile([P, 2, C], F32, name="dx_ps", tag=tag)
+            for i in range(2):
+                cols = slice((2 * half + i) * P, (2 * half + i + 1) * P)
                 nc.tensor.matmul_mx(
-                    out=dx_ps[e][b // 2][:, b % 2, :], lhsT=w1t[e][:, cols].bitcast(FP8X4),
+                    out=dx_ps[e][half][:, i, :], lhsT=w1t[e][:, cols].bitcast(FP8X4),
                     lhsT_scale=w1t_plane[4 * e :, cols],
                     rhs=da_q[:].bitcast(FP8X4), rhs_scale=da_s[:], start=True, stop=True,
                 )
-            hand_out(e, 0)
 
         front(0)
         gather(rest, "xs", "slope0", C, S)
-        back(0)
-        front(1)
-        front(2)
-        back(1)
-        front(3)
-        back(2)
-        back(3)
+        for e in range(E):
+            turn(e)
+            if e > 0:
+                hand_out(e - 1, 1)
+            back(e, 0)
+            hand_out(e, 0)
+            if e + 1 < E:
+                front(e + 1)
+            back(e, 1)
         hand_out(E - 1, 1)

@@ -130,12 +130,12 @@ def tile_moe_rec_mlp_relu2_kernel(
             x_g, xs_g, dys_g = part["x"], part["xs"], part["dys"]
             dy_g = [part["dy0"], part["dy1"]]
             slots = slice(0, C) if e == 0 else slice((e - 1) * C, e * C)
-            a_ps = psum.tile([P, H], F32, name="a_ps", tag="first_half1" if e == 0 else "second_half")
+            a_ps = psum.tile([P, H], F32, name="a_ps", tag="first_half1" if e == 0 else "bank_a")
             nc.tensor.matmul_mx(
                 out=a_ps[:], lhsT=x_g[:, slots].bitcast(FP8X4), lhsT_scale=xs_g[:, slots],
                 rhs=w1[e][:].bitcast(FP8X4), rhs_scale=w1_plane[4 * e :, :], start=True, stop=True,
             )
-            dh_ps = psum.tile([P, H], F32, name="dh_ps", tag=f"dh{e}" if e < 2 else f"first_half{e % 2}")
+            dh_ps = psum.tile([P, H], F32, name="dh_ps", tag=f"dh{min(e, 1)}")
             for s in range(N_PASSES):
                 nc.tensor.matmul_mx(
                     out=dh_ps[:], lhsT=dy_g[s][:, slots].bitcast(FP8X4), lhsT_scale=dys_g[4 * s :, slots],
@@ -143,10 +143,18 @@ def tile_moe_rec_mlp_relu2_kernel(
                     rhs_scale=w2_planes[e // 2][4 * (2 * (e % 2) + s) :, :],
                     start=(s == 0), stop=(s == N_PASSES - 1),
                 )
+            if e >= 2:
+                dh = ring.tile([P, H], F32, name="dh")
+                nc.scalar.activation(dh[:], dh_ps[:], COPY, scale=gate_col[:, e : e + 1])
             slope = keep.tile([P, H], F32, name=f"slope{e}", tag=f"slope{e}", align_bytes=64)
             nc.scalar.activation(slope[:], a_ps[:], RELU, scale=2.0)
             da_t[e] = keep.tile([P, H], BF16, name=f"da_t{e}", tag=f"da_t{e}")
-            nc.vector.scalar_tensor_tensor(da_t[e][:], dh_ps[:], gate_col[:, e : e + 1], slope[:], MULT, MULT)
+            if e < 2:
+                nc.vector.scalar_tensor_tensor(
+                    da_t[e][:], dh_ps[:], gate_col[:, e : e + 1], slope[:], MULT, MULT
+                )
+            else:
+                nc.gpsimd.tensor_tensor(da_t[e][:], dh[:], slope[:], MULT)
 
         def hand_out(e, half):
             tag = f"da_t{e + 1}" if half == 1 and e + 1 < E else f"dx_{e}_{half}"
@@ -164,7 +172,7 @@ def tile_moe_rec_mlp_relu2_kernel(
 
         def turn(e):
             pairs = da_t[e][:].bitcast(F32)
-            turned = psum.tile([P, 2, P], F32, name="turned", tag="second_half" if e == 0 else f"bank_t{e % 2}")
+            turned = psum.tile([P, 2, P], F32, name="turned", tag="bank_a" if e == 0 else f"bank_t{e % 2}")
             for u in range(2):
                 nc.tensor.transpose(turned[:, u, :], pairs[:, u : H // 2 : 2], identity[:])
             da = ring.tile([P, 4 * C], BF16, name="da", align_bytes=64)
@@ -179,7 +187,7 @@ def tile_moe_rec_mlp_relu2_kernel(
 
         def back(e, half):
             da_q, da_s = da_mx[e]
-            tag = "second_half" if half == 1 else f"first_half{e % 2}"
+            tag = "second_half" if half == 1 else ("bank_a" if 0 < e < E - 1 else "first_half0")
             dx_ps[e][half] = psum.tile([P, 2, C], F32, name="dx_ps", tag=tag)
             for i in range(2):
                 cols = slice((2 * half + i) * P, (2 * half + i + 1) * P)
@@ -195,9 +203,11 @@ def tile_moe_rec_mlp_relu2_kernel(
             turn(e)
             if e > 0:
                 hand_out(e - 1, 1)
+            if 0 < e < E - 1:
+                front(e + 1)
             back(e, 0)
             hand_out(e, 0)
-            if e + 1 < E:
-                front(e + 1)
+            if e == 0:
+                front(1)
             back(e, 1)
         hand_out(E - 1, 1)

from contextlib import ExitStack

import concourse.mybir as mybir
from concourse.masks import make_identity

K, T, E, C, H, N = 512, 512, 4, 128, 512, 1024
FLOPS = 2 * E * C * (K * H + N * H + H * K)

F32 = mybir.dt.float32
BF16 = mybir.dt.bfloat16
I32 = mybir.dt.int32
U32 = mybir.dt.uint32
U16 = mybir.dt.uint16
U8 = mybir.dt.uint8
FP8X4 = mybir.dt.float8_e4m3fn_x4
MULT = mybir.AluOpType.mult
RELU = mybir.ActivationFunctionType.Relu
COPY = mybir.ActivationFunctionType.Copy

P = 128
S = E * C
N_PASSES = N // 512
K_BLOCKS = K // P


def tile_moe_rec_mlp_relu2_kernel(
    tc, x_words, x_scales, dy_words, dy_scales, w1_words, w1_scales,
    w2t_words, w2t_scales, w1t_words, w1t_scales, gate, offs, out,
):
    nc = tc.nc

    with ExitStack() as ctx:
        keep = ctx.enter_context(tc.tile_pool(name="keep", bufs=1))
        ring = ctx.enter_context(tc.tile_pool(name="ring", bufs=2))
        psum = ctx.enter_context(tc.psum_pool(name="psum", bufs=1))

        offsets = keep.tile([P, S // 16], U16, name="offsets")

        def plane(name, engine):
            t = keep.tile([P, 512], U8, name=name, align_bytes=64)
            engine.memset(t[:].bitcast(I32), 0)
            return t

        def load_plane(t, rows, quadrants=range(4), engine=nc.sync):
            n = rows.shape[0]
            for q in quadrants:
                engine.dma_start(
                    out=t[32 * q : 32 * q + 4 * n, :].bitcast(I32),
                    in_=rows[:, 4 * q : 4 * q + 4, :].bitcast(I32),
                )

        def load_words(name, words, dtype):
            n = words.shape[0]
            t = keep.tile([P, n * 512], dtype, name=name, align_bytes=64)
            nc.sync.dma_start(
                out=t[:].bitcast(I32).rearrange("p (s c) -> p s c", s=n),
                in_=words.rearrange("s p c d -> p s (c d)").bitcast(I32),
            )
            return t

        x_plane = keep.tile([P, 512], U8, name="x_plane", align_bytes=64)
        dy_plane = plane("dy_plane", nc.gpsimd)
        w1_plane = plane("w1_plane", nc.gpsimd)
        w2_planes = [plane("w2_plane0", nc.gpsimd)]
        w1_rows = w1_scales.rearrange("e s b c -> (e s) b c")
        w2_rows = w2t_scales.rearrange("e s b c -> (e s) b c")
        gate_rows = keep.tile([P, C], F32, name="gate_rows")
        nc.gpsimd.dma_start(out=gate_rows[:], in_=gate[: P // E, :].rearrange("r (e c) -> (r e) c", e=E))
        identity = keep.tile([P, P], F32, name="identity")
        nc.vector.memset(identity[:], 0.0)
        make_identity(nc, identity[:], nomemset=True)
        load_plane(w2_planes[0], w2_rows[0:4], engine=nc.gpsimd)

        w1t_plane = plane("w1t_plane", nc.vector)
        w2_planes.append(plane("w2_plane1", nc.vector))

        nc.sync.dma_start(offsets[:], offs)
        x_all = load_words("x_all", x_words, I32)
        for q in range(4):
            nc.sync.dma_start(
                out=x_plane[32 * q : 32 * q + 32, :].bitcast(I32),
                in_=x_scales[0, 4 * q : 4 * q + 4, :].bitcast(I32).partition_broadcast(8),
            )
        dy_all = load_words("dy_all", dy_words, I32)
        w1, w2, w1t = [], [], []
        w1.append(load_words("w1_0", w1_words[0], U32))
        load_plane(dy_plane, dy_scales)
        load_plane(w1_plane, w1_rows, range(1))
        w2.append(load_words("w2_0", w2t_words[0], U32))
        load_plane(w1_plane, w1_rows, range(1, 4))
        for e in range(1, E):
            w2.append(load_words(f"w2_{e}", w2t_words[e], U32))
            w1.append(load_words(f"w1_{e}", w1_words[e], U32))
            if e == 2:
                load_plane(w2_planes[1], w2_rows[4:8])
            w1t.append(load_words(f"w1t_{e - 1}", w1t_words[e - 1], U32))
            if e == 1:
                load_plane(w1t_plane, w1t_scales.rearrange("e s b c -> (e s) b c"))
        w1t.append(load_words(f"w1t_{E - 1}", w1t_words[E - 1], U32))

        gate_ps = psum.tile([P, 2, P], F32, name="gate_ps", tag="bank_t1")
        nc.tensor.transpose(gate_ps[:, 0, :], gate_rows[:], identity[:])
        gate_col = keep.tile([P, E], F32, name="gate_col")
        nc.scalar.activation(gate_col[:], gate_ps[:, 0, 0:E], COPY)

        windows = {
            "x": (x_all[:].bitcast(U32), U32),
            "xs": (x_plane[:], U8),
            "dys": (dy_plane[:], U8),
            "dy0": (dy_all[:, 0:T].bitcast(U32), U32),
            "dy1": (dy_all[:, T : 2 * T].bitcast(U32), U32),
        }
        first, rest = {}, {}

        def gather(part, sort, tag, lo, hi):
            window, dtype = windows[sort]
            part[sort] = keep.tile([P, hi - lo], dtype, name=f"{sort}_{lo}", tag=tag, align_bytes=64)
            nc.vector.tensor_copy(part[sort][:], window.indirect(offsets[:, lo // 16 : hi // 16]))

        for sort in windows:
            gather(first, sort, f"{sort}_first", 0, C)
        for sort in ("x", "dy0", "dy1", "dys"):
            gather(rest, sort, f"{sort}_rest", C, S)

        dx_tokens = [keep.tile([P, T], F32, name=f"dx_tokens{b}") for b in range(K_BLOCKS)]
        da_t, dx_ps = {}, {}

        def front(e):
            part = first if e == 0 else rest
            x_g, xs_g, dys_g = part["x"], part["xs"], part["dys"]
            dy_g = [part["dy0"], part["dy1"]]
            slots = slice(0, C) if e == 0 else slice((e - 1) * C, e * C)
            a_ps = psum.tile([P, H], F32, name="a_ps", tag="first_half1" if e == 0 else "bank_a")
            nc.tensor.matmul_mx(
                out=a_ps[:], lhsT=x_g[:, slots].bitcast(FP8X4), lhsT_scale=xs_g[:, slots],
                rhs=w1[e][:].bitcast(FP8X4), rhs_scale=w1_plane[4 * e :, :], start=True, stop=True,
            )
            dh_ps = psum.tile([P, H], F32, name="dh_ps", tag=f"dh{min(e, 1)}")
            for s in range(N_PASSES):
                nc.tensor.matmul_mx(
                    out=dh_ps[:], lhsT=dy_g[s][:, slots].bitcast(FP8X4), lhsT_scale=dys_g[4 * s :, slots],
                    rhs=w2[e][:, s * H : (s + 1) * H].bitcast(FP8X4),
                    rhs_scale=w2_planes[e // 2][4 * (2 * (e % 2) + s) :, :],
                    start=(s == 0), stop=(s == N_PASSES - 1),
                )
            if e >= 2:
                dh = ring.tile([P, H], F32, name="dh")
                nc.scalar.activation(dh[:], dh_ps[:], COPY, scale=gate_col[:, e : e + 1])
            slope = keep.tile([P, H], F32, name=f"slope{e}", tag=f"slope{e}", align_bytes=64)
            nc.scalar.activation(slope[:], a_ps[:], RELU, scale=2.0)
            da_t[e] = keep.tile([P, H], BF16, name=f"da_t{e}", tag=f"da_t{e}")
            if e < 2:
                nc.vector.scalar_tensor_tensor(
                    da_t[e][:], dh_ps[:], gate_col[:, e : e + 1], slope[:], MULT, MULT
                )
            else:
                nc.gpsimd.tensor_tensor(da_t[e][:], dh[:], slope[:], MULT)

        def hand_out(e, half):
            tag = f"da_t{e + 1}" if half == 1 and e + 1 < E else f"dx_{e}_{half}"
            staged = keep.tile([P, 2, C], F32, name=f"dx_{e}_{half}", tag=tag)
            nc.scalar.copy(staged[:], dx_ps[e][half][:])
            for i in range(2):
                b = 2 * half + i
                nc.vector.tensor_copy(
                    dx_tokens[b][:].indirect(offsets[:, e * C // 16 : (e + 1) * C // 16]), staged[:, i, :]
                )
                if e == E - 1:
                    nc.sync.dma_start(out=out[b * P : (b + 1) * P, :], in_=dx_tokens[b][:])

        da_mx = {}

        def turn(e):
            pairs = da_t[e][:].bitcast(F32)
            turned = psum.tile([P, 2, P], F32, name="turned", tag="bank_a" if e == 0 else f"bank_t{e % 2}")
            for u in range(2):
                nc.tensor.transpose(turned[:, u, :], pairs[:, u : H // 2 : 2], identity[:])
            da = ring.tile([P, 4 * C], BF16, name="da", align_bytes=64)
            nc.scalar.copy(
                da[:].bitcast(F32).rearrange("p (j u) -> p j u", u=2), turned[:].rearrange("p u j -> p j u")
            )
            da_q = ring.tile([P, C], U32, name="da_q", align_bytes=64)
            da_s = ring.tile([P, C], U8, name="da_s", align_bytes=64)
            nc.vector.quantize_mx(out=da_q[:].bitcast(FP8X4), scales=da_s[:], in_=da[:])
            da_mx[e] = (da_q, da_s)
            dx_ps[e] = {}

        def back(e, half):
            da_q, da_s = da_mx[e]
            tag = "second_half" if half == 1 else ("bank_a" if 0 < e < E - 1 else "first_half0")
            dx_ps[e][half] = psum.tile([P, 2, C], F32, name="dx_ps", tag=tag)
            for i in range(2):
                cols = slice((2 * half + i) * P, (2 * half + i + 1) * P)
                nc.tensor.matmul_mx(
                    out=dx_ps[e][half][:, i, :], lhsT=w1t[e][:, cols].bitcast(FP8X4),
                    lhsT_scale=w1t_plane[4 * e :, cols],
                    rhs=da_q[:].bitcast(FP8X4), rhs_scale=da_s[:], start=True, stop=True,
                )

        front(0)
        gather(rest, "xs", "slope0", C, S)
        for e in range(E):
            turn(e)
            if e > 0:
                hand_out(e - 1, 1)
            if 0 < e < E - 1:
                front(e + 1)
            back(e, 0)
            hand_out(e, 0)
            if e == 0:
                front(1)
            back(e, 1)
        hand_out(E - 1, 1)
